import numpy as np
import ml_dtypes


def mxq(x, axis, fmt="e4m3"):
    dtype, down = {"e4m3": (ml_dtypes.float8_e4m3fn, 7), "e5m2": (ml_dtypes.float8_e5m2, 14)}[fmt]
    v = np.moveaxis(np.asarray(x, np.float32).astype(ml_dtypes.bfloat16).astype(np.float64), axis, -1)
    blocks = v.reshape(v.shape[:-1] + (-1, 32))
    amax = np.abs(blocks).max(-1, keepdims=True)
    byte = np.maximum(np.where(amax > 0, np.frexp(amax)[1] - 1 + 127, 0) - down, 1)
    scale = np.exp2(byte - 127.0)
    codes = (blocks / scale).astype(np.float32).astype(dtype).astype(np.float64)
    return np.moveaxis((codes * scale).reshape(v.shape), -1, axis)


WIDE = False


def mx_kscale(k):
    if not WIDE:
        return np.ones(k)
    levels = np.array([30, -30])
    if k % 512:
        return np.exp2(np.random.permutation(np.resize(levels, k // 32))).repeat(32)
    a = np.empty((k // 512, 16))
    for p in range(k // 512):
        a[p, :8] = np.random.permutation(np.resize(levels, 8))
        for g in range(8):
            far = levels[np.abs(levels - a[p, g]) >= 10]
            a[p, g + 8] = far[np.random.randint(len(far))]
    return np.exp2(a.ravel()).repeat(32)


def f64(x):
    return np.asarray(x).astype(np.float64)


def striped(idx):
    return np.tile(np.asarray(idx).reshape(-1, 16).T, (8, 1)).astype(np.uint16)


def unstriped(offs):
    return offs[:16].T.reshape(-1).astype(np.int64)


def striped8(idx):
    return np.asarray(idx).reshape(8, -1, 16).transpose(0, 2, 1).reshape(128, -1).astype(np.uint16)


def unstriped8(offs):
    return offs.reshape(8, 16, -1).transpose(0, 2, 1).reshape(8, -1).astype(np.int64)


def pick8(x, idx, run):
    r = np.arange(len(x))
    return x[r[:, None], idx[r % (8 * run) // run]]


E2M1 = np.array([0.0, 0.5, 1.0, 1.5, 2.0, 3.0, 4.0, 6.0, -0.0, -0.5, -1.0, -1.5, -2.0, -3.0, -4.0, -6.0])


def pack_weight(w, fmt):
    k, n = w.shape
    w = f64(np.asarray(w, np.float32).astype(ml_dtypes.bfloat16)).reshape(k // 32, 32, n)
    amax = np.abs(w).max(1)
    if fmt in ("e4m3", "e5m2"):
        byte = np.frexp(amax)[1] - 1 + 127 - (7 if fmt == "e4m3" else 14)
    else:
        mant, ex = np.frexp(amax / 6.0)
        byte = np.where(mant > 0.5, ex, ex - 1) + 127
    byte = np.clip(np.where(amax > 0, byte, 1), 1, 254)
    scaled = (w * np.exp2(127.0 - byte)[:, None, :]).reshape(k, n).astype(np.float32)
    by_word = np.ascontiguousarray(scaled.reshape(k // 512, 128, 4, n).transpose(0, 1, 3, 2))
    if fmt in ("e4m3", "e5m2"):
        words = by_word.astype(ml_dtypes.float8_e4m3fn if fmt == "e4m3" else ml_dtypes.float8_e5m2).view(np.uint8)
    else:
        c = by_word.astype(ml_dtypes.float4_e2m1fn).view(np.uint8) & 0xF
        words = (c[..., 0::2] | (c[..., 1::2] << 4)).reshape(k // 512, 128, 2 * n)
    return np.ascontiguousarray(words), np.ascontiguousarray(byte.astype(np.uint8).reshape(k // 512, 16, n))


def unpack_weight(words, scales, fmt):
    g, _, n = scales.shape
    words = np.ascontiguousarray(words).reshape(g, 128, n, -1)
    if fmt in ("e4m3", "e5m2"):
        vals = words.view(ml_dtypes.float8_e4m3fn if fmt == "e4m3" else ml_dtypes.float8_e5m2).astype(np.float64)
    else:
        nib = np.empty((g, 128, n, 4), np.uint8)
        nib[..., 0::2] = words & 0xF
        nib[..., 1::2] = words >> 4
        vals = E2M1[nib]
    vals = vals * np.repeat(np.exp2(scales.astype(np.float64) - 127.0), 8, axis=1)[..., None]
    return vals.transpose(0, 1, 3, 2).reshape(g * 512, n)


def sigmoid(v):
    return 1.0 / (1.0 + np.exp(-v))


def sgn(shape):
    return np.random.uniform(0.5, 2.0, shape) * np.where(np.random.standard_normal(shape) < 0, -1.0, 1.0)


K, T, J, R, C, N = 512, 1024, 256, 512, 512, 256


def setup_inputs():
    n = np.random.standard_normal
    idx = np.random.permutation(T)[:J]
    idx2 = np.stack([np.random.permutation(C)[:J] for _ in range(8)])
    idx3 = np.stack([np.random.permutation(C)[:J] for _ in range(8)])
    fk = mx_kscale(K)
    fr = mx_kscale(R)
    xtp = pack_weight(n((K, T)) / fk[:, None], "e4m3")
    wp = pack_weight(n((K, R)) * 1 / np.sqrt(K) * fk[:, None] * fr, "e2m1")
    w2p = pack_weight(n((K, R)) * 1 / np.sqrt(K) * fk[:, None], "e5m2")
    wbp = pack_weight(n((R, N)) * 1 / np.sqrt(R) / fr[:, None], "e5m2")
    return {
        "xt_words": xtp[0],
        "xt_scales": xtp[1],
        "w_words": wp[0],
        "w_scales": wp[1],
        "w2_words": w2p[0],
        "w2_scales": w2p[1],
        "sg": (sgn((R, 1))).astype(np.float32),
        "bg": (np.random.uniform(-2.0, 2.0, (R, 1))).astype(np.float32),
        "wb_words": wbp[0],
        "wb_scales": wbp[1],
        "offs": striped(idx),
        "offs2": striped8(idx2),
        "offs3": striped8(idx3),
    }


def reference(xt_words, xt_scales, w_words, w_scales, w2_words, w2_scales, sg, bg, wb_words, wb_scales, offs, offs2, offs3):
    idx = unstriped(offs)
    idx2 = unstriped8(offs2)
    idx3 = unstriped8(offs3)
    xtu = unpack_weight(xt_words, xt_scales, "e4m3")
    wu = unpack_weight(w_words, w_scales, "e2m1")
    w2u = unpack_weight(w2_words, w2_scales, "e5m2")
    wbu = unpack_weight(wb_words, wb_scales, "e5m2")
    xtidxg = xtu[:, idx]
    a = wu.T @ xtidxg
    b = w2u.T @ xtidxg
    pa = np.zeros((R, C))
    pa[np.arange(R)[:, None], idx2[np.arange(R) % 512 // 64]] = a
    pb = np.zeros((R, C))
    pb[np.arange(R)[:, None], idx3[np.arange(R) % 512 // 64]] = b
    hid = pa * sigmoid(pb * f64(sg) + f64(bg))
    hidq = mxq(hid, 0, "e4m3")
    p = wbu.T @ hidq
    return p

@@ -1,0 +1,226 @@
+from contextlib import ExitStack
+
+import concourse.mybir as mybir
+
+K, T, J, R, C, N = 512, 1024, 256, 512, 512, 256
+FLOPS = 2 * (2 * K * R * J + R * N * C)
+
+F32 = mybir.dt.float32
+BF16 = mybir.dt.bfloat16
+I32 = mybir.dt.int32
+U32 = mybir.dt.uint32
+U16 = mybir.dt.uint16
+U8 = mybir.dt.uint8
+E4M3 = mybir.dt.float8_e4m3fn_x4
+E5M2 = mybir.dt.float8_e5m2_x4
+E2M1 = mybir.dt.float4_e2m1fn_x4
+COPY = mybir.ActivationFunctionType.Copy
+SIGMOID = mybir.ActivationFunctionType.Sigmoid
+MULT = mybir.AluOpType.mult
+
+P = 128
+PACK = 4
+QUADS = 4
+HALF = J // 2
+CHUNKS = ((0, 128), (128, 384), (384, 512))
+
+
+def tile_list_gatedboards_kernel(
+    tc, xt_words, xt_scales, w_words, w_scales, w2_words, w2_scales, sg, bg, wb_words, wb_scales, offs, offs2, offs3, out
+):
+    nc = tc.nc
+    with ExitStack() as ctx:
+        keep = ctx.enter_context(tc.tile_pool(name="keep", bufs=1))
+        psum = ctx.enter_context(tc.psum_pool(name="psum", bufs=8))
+
+        def tile(shape, dtype, name, on=None):
+            return keep.tile(shape, dtype, name=name, tag=on or name, align_bytes=64)
+
+        def words_of(dram):
+            return dram[0].rearrange("p c r -> p (c r)").bitcast(I32)
+
+        def zeroed_plane(width, name):
+            plane = tile([P, width], U8, name)
+            nc.vector.memset(plane[:].bitcast(I32), 0)
+            return plane
+
+        def load_plane(queue, plane, dram):
+            for q in range(QUADS):
+                queue.dma_start(out=plane[32 * q : 32 * q + 4, :].bitcast(I32), in_=dram[0, 4 * q : 4 * q + 4, :].bitcast(I32))
+
+        def load_list(dram, name):
+            offsets = tile([P, J // 16], U16, name)
+            nc.sync.dma_start(out=offsets[:], in_=dram)
+            return offsets
+
+        xs = zeroed_plane(T, "xs")
+        ws_two = zeroed_plane(2 * R, "ws_two")
+
+        idx = load_list(offs, "idx")
+        ws_rows = tile([4, QUADS, R // 4], I32, "ws_rows")
+        nc.scalar.dma_start(out=ws_rows[:], in_=w_scales[0].bitcast(I32).rearrange("(q r) c -> r q c", r=4))
+        xw = tile([P, T], I32, "xw")
+        nc.scalar.dma_start(out=xw[:], in_=words_of(xt_words))
+        load_plane(nc.sync, xs, xt_scales)
+        w_raw = tile([P, R], U16, "w_raw")
+        nc.sync.dma_start(out=w_raw[:].bitcast(I32), in_=w_words[0].bitcast(I32))
+        idx2 = load_list(offs2, "idx2")
+        w2_raw = tile([P, R], I32, "w2_raw")
+        nc.sync.dma_start(out=w2_raw[:], in_=words_of(w2_words))
+        w2s_plane = zeroed_plane(R, "w2s_plane")
+        load_plane(nc.sync, w2s_plane, w2_scales)
+        idx3 = load_list(offs3, "idx3")
+        slope = tile([P, PACK], F32, "slope")
+        nc.sync.dma_start(out=slope[:], in_=sg.rearrange("(p t) o -> p (t o)", t=PACK))
+        offset = tile([P, PACK], F32, "offset")
+        nc.sync.dma_start(out=offset[:], in_=bg.rearrange("(p t) o -> p (t o)", t=PACK))
+        wb = tile([P, N], I32, "wb")
+        nc.sync.dma_start(out=wb[:], in_=words_of(wb_words))
+        wbs = zeroed_plane(N, "wbs")
+        load_plane(nc.sync, wbs, wb_scales)
+
+        def new_board(name, on=None):
+            board = tile([P, C], F32, name, on)
+            nc.vector.memset(board[:], 0.0)
+            return board
+
+
+        def deal(engine_copy, raw, dtype, name, t0, t1, on=None):
+            dealt = tile([P, t1 - t0, P], dtype, name, on)
+            engine_copy(out=dealt[:], in_=raw[:].rearrange("p (m t) -> p t m", t=PACK)[:, t0:t1, :])
+            return dealt
+
+        ws_words = ws_two[:].bitcast(I32).rearrange("p (h c) -> p h c", h=2)
+        for low in range(2):
+            nc.vector.tensor_copy(out=ws_words[32 * low : 32 * low + 4, :, :], in_=ws_rows[:, low:QUADS:2, :])
+        nc.vector.tensor_copy(out=ws_words[64:128, 0, :], in_=ws_words[0:64, 1, :])
+        ws_plane = ws_two[:, 0:R]
+        w_lo = [deal(nc.scalar.copy, w_raw, U16, "w%d" % t, t, t + 1) for t in range(2)]
+        ws_lo = deal(nc.vector.tensor_copy, ws_plane, U8, "ws_lo", 0, 2)
+        w_hi = deal(nc.scalar.copy, w_raw, U16, "w_hi", 2, 4)
+
+        xg = tile([P, J], U32, "xg")
+        xgs = tile([P, J], U8, "xgs")
+
+        def gather(j0, j1):
+            entries = idx[:, j0 // 16 : j1 // 16]
+            nc.vector.tensor_copy(out=xg[:, j0:j1], in_=xw[:].bitcast(U32).indirect(entries))
+            nc.vector.tensor_copy(out=xgs[:, j0:j1], in_=xs[:].indirect(entries))
+
+        def sums(operands, j0, j1, name):
+            acc = psum.tile([P, len(operands), j1 - j0], F32, name="acc_" + name, tag="acc")
+            for u, (words, scales) in enumerate(operands):
+                nc.tensor.matmul_mx(
+                    out=acc[:, u, :], lhsT=words, lhsT_scale=scales, rhs=xg[:, j0:j1].bitcast(E4M3), rhs_scale=xgs[:, j0:j1],
+                    start=True, stop=True,
+                )
+            return acc
+
+        def leave_psum(acc, name):
+            result = tile(list(acc.shape), F32, name)
+            nc.vector.tensor_copy(out=result[:], in_=acc[:])
+            return [result[:, u, :] for u in range(acc.shape[1])]
+
+        def products(operands, j0, j1, name):
+            return leave_psum(sums(operands, j0, j1, name), name)
+
+        def scatter(board, offsets, values, j0, j1):
+            nc.scalar.activation(out=board[:].indirect(offsets[:, j0 // 16 : j1 // 16]), in_=values, func=COPY)
+
+        halves = ((0, HALF), (HALF, J))
+        pa = [new_board("pa0"), new_board("pa1")]
+        for j0, j1 in halves:
+            gather(j0, j1)
+            for t in range(2):
+                (a,) = products([(w_lo[t][:, 0, :].bitcast(E2M1), ws_lo[:, t, :])], j0, j1, "a%d_%d" % (t, j0))
+                scatter(pa[t], idx2, a, j0, j1)
+
+        w2 = tile([P, PACK, P], I32, "w2")
+        nc.vector.tensor_copy(
+            out=w2[:].rearrange("p t (g i) -> p g t i", i=4), in_=w2_raw[:].rearrange("p (g i t) -> p g t i", i=4, t=PACK)
+        )
+        w2s = deal(nc.vector.tensor_copy, w2s_plane, U8, "w2s", 0, PACK)
+        ws_hi = deal(nc.vector.tensor_copy, ws_plane, U8, "ws_hi", 2, 4, on="w2s_plane")
+        pb = [new_board("pb0"), new_board("pb1"), new_board("pb2", on="w1")]
+
+        def first(t):
+            return w_hi[:, t - 2, :].bitcast(E2M1), ws_hi[:, t - 2, :]
+
+        def second(t):
+            return w2[:, t, :].bitcast(E5M2), w2s[:, t, :]
+
+        b0, b1 = products([second(0), second(1)], 0, J, "b01")
+        (b2,) = products([second(2)], 0, J, "b2")
+        (a2,) = products([first(2)], 0, J, "a2")
+        last_sums = sums([second(3), first(3)], 0, J, "b3a3")
+        pa.append(new_board("pa2", on="w2"))
+        pb.append(new_board("pb3", on="w_hi"))
+        pa.append(new_board("pa3", on="w2s_plane"))
+        b3, a3 = leave_psum(last_sums, "b3a3")
+        hid = [tile([P, c1 - c0, PACK], BF16, "hid%d" % c0) for c0, c1 in CHUNKS]
+        gates = []
+
+        def gate(t):
+            g = tile([P, C], F32, "gate%d" % t)
+            nc.scalar.activation(out=g[:], in_=pb[t][:], func=SIGMOID, bias=offset[:, t : t + 1], scale=slope[:, t : t + 1])
+            gates.append(g)
+
+        def gated(t):
+            for h, (c0, c1) in zip(hid, CHUNKS):
+                nc.vector.tensor_tensor(out=h[:, :, t], in0=pa[t][:, c0:c1], in1=gates[t][:, c0:c1], op=MULT)
+
+        for t, values in enumerate((b0, b1, b2)):
+            scatter(pb[t], idx3, values, 0, J)
+        for t in range(3):
+            gate(t)
+        scatter(pa[2], idx2, a2, 0, J)
+        for t in range(3):
+            gated(t)
+        scatter(pb[3], idx3, b3, 0, J)
+        scatter(pa[3], idx2, a3, 0, J)
+
+        last = PACK - 1
+        rows_last = []
+
+        def last_row(i):
+            c0, c1 = CHUNKS[i]
+            g = tile([P, c1 - c0], F32, "gate_last%d" % i)
+            nc.scalar.activation(
+                out=g[:], in_=pb[last][:, c0:c1], func=SIGMOID, bias=offset[:, last : last + 1], scale=slope[:, last : last + 1]
+            )
+            row = tile([P, c1 - c0], BF16, "row%d" % i)
+            nc.vector.tensor_tensor(out=row[:], in0=pa[last][:, c0:c1], in1=g[:], op=MULT)
+            rows_last.append(row)
+
+        def weave(i):
+            nc.vector.tensor_copy(out=hid[i][:, :, last], in_=rows_last[i][:])
+
+        def finish(i):
+            c0, c1 = CHUNKS[i]
+            codes = tile([P, c1 - c0], U32, "codes%d" % i)
+            scales = tile([P, c1 - c0], U8, "scales%d" % i)
+            nc.vector.quantize_mx(out=codes[:].bitcast(E4M3), scales=scales[:], in_=hid[i][:].rearrange("p c t -> p (c t)"))
+            for u in range(N // P):
+                rows = slice(u * P, (u + 1) * P)
+                acc = psum.tile([P, c1 - c0], F32, name="out_acc%d_%d" % (i, u), tag="acc")
+                nc.tensor.matmul_mx(
+                    out=acc[:], lhsT=wb[:, rows].bitcast(E5M2), lhsT_scale=wbs[:, rows], rhs=codes[:].bitcast(E4M3), rhs_scale=scales[:],
+                    start=True, stop=True,
+                )
+                result = tile([P, c1 - c0], F32, "result%d_%d" % (i, u))
+                if i == len(CHUNKS) - 1 and u == 0:
+                    nc.vector.tensor_copy(out=result[:], in_=acc[:])
+                else:
+                    nc.scalar.copy(out=result[:], in_=acc[:])
+                queue = nc.scalar if (i == len(CHUNKS) - 1 and u == 1) else nc.sync
+                queue.dma_start(out=out[rows, c0:c1], in_=result[:])
+
+        last_row(0)
+        last_row(1)
+        weave(0)
+        last_row(2)
+        weave(1)
+        finish(0)
+        weave(2)
+        finish(1)
+        finish(2)

@@ -64,6 +64,10 @@ def tile_list_gatedboards_kernel(
         load_plane(nc.sync, xs, xt_scales)
         w_raw = tile([P, R], U16, "w_raw")
         nc.sync.dma_start(out=w_raw[:].bitcast(I32), in_=w_words[0].bitcast(I32))
+        zero = tile([P, 1], F32, "zero")
+        nc.gpsimd.memset(zero[:], 0.0)
+        unused = tile([P, 1], F32, "unused")
+        nc.scalar.activation(out=unused[:], in_=zero[:], func=SIGMOID)
         idx2 = load_list(offs2, "idx2")
         w2_raw = tile([P, R], I32, "w2_raw")
         nc.sync.dma_start(out=w2_raw[:], in_=words_of(w2_words))

@@ -22,7 +22,8 @@ P = 128
 PACK = 4
 QUADS = 4
 HALF = J // 2
-CHUNKS = ((0, 128), (128, 384), (384, 512))
+CHUNK = 128
+CHUNKS = C // CHUNK
 
 
 def tile_list_gatedboards_kernel(
@@ -139,92 +140,81 @@ def tile_list_gatedboards_kernel(
                 (a,) = products([(w_lo[t][:, 0, :].bitcast(E2M1), ws_lo[:, t, :])], j0, j1, "a%d_%d" % (t, j0))
                 scatter(pa[t], idx2, a, j0, j1)
 
+        ws_hi = deal(nc.vector.tensor_copy, ws_plane, U8, "ws_hi", 2, 4, on="xs")
+        pa.append(new_board("pa2", on="w0"))
+        a2, a3 = products([(w_hi[:, u, :].bitcast(E2M1), ws_hi[:, u, :]) for u in range(2)], 0, J, "a23")
+        scatter(pa[2], idx2, a2, 0, J)
+
         w2 = tile([P, PACK, P], I32, "w2")
         nc.vector.tensor_copy(
             out=w2[:].rearrange("p t (g i) -> p g t i", i=4), in_=w2_raw[:].rearrange("p (g i t) -> p g t i", i=4, t=PACK)
         )
         w2s = deal(nc.vector.tensor_copy, w2s_plane, U8, "w2s", 0, PACK)
-        ws_hi = deal(nc.vector.tensor_copy, ws_plane, U8, "ws_hi", 2, 4, on="w2s_plane")
-        pb = [new_board("pb0"), new_board("pb1"), new_board("pb2", on="w1")]
+        pb = [new_board("pb%d" % t, on=on) for t, on in enumerate(("w1", "w_hi", "xs"))]
+        b = []
+        for t in (0, 2):
+            b.extend(products([(w2[:, t + u, :].bitcast(E5M2), w2s[:, t + u, :]) for u in range(2)], 0, J, "b%d" % t))
 
-        def first(t):
-            return w_hi[:, t - 2, :].bitcast(E2M1), ws_hi[:, t - 2, :]
-
-        def second(t):
-            return w2[:, t, :].bitcast(E5M2), w2s[:, t, :]
-
-        b0, b1 = products([second(0), second(1)], 0, J, "b01")
-        (b2,) = products([second(2)], 0, J, "b2")
-        (a2,) = products([first(2)], 0, J, "a2")
-        last_sums = sums([second(3), first(3)], 0, J, "b3a3")
-        pa.append(new_board("pa2", on="w2"))
-        pb.append(new_board("pb3", on="w_hi"))
-        pa.append(new_board("pa3", on="w2s_plane"))
-        b3, a3 = leave_psum(last_sums, "b3a3")
-        hid = [tile([P, c1 - c0, PACK], BF16, "hid%d" % c0) for c0, c1 in CHUNKS]
-        gates = []
-
-        def gate(t):
-            g = tile([P, C], F32, "gate%d" % t)
-            nc.scalar.activation(out=g[:], in_=pb[t][:], func=SIGMOID, bias=offset[:, t : t + 1], scale=slope[:, t : t + 1])
-            gates.append(g)
-
-        def gated(t):
-            for h, (c0, c1) in zip(hid, CHUNKS):
-                nc.vector.tensor_tensor(out=h[:, :, t], in0=pa[t][:, c0:c1], in1=gates[t][:, c0:c1], op=MULT)
-
-        for t, values in enumerate((b0, b1, b2)):
-            scatter(pb[t], idx3, values, 0, J)
-        for t in range(3):
-            gate(t)
-        scatter(pa[2], idx2, a2, 0, J)
-        for t in range(3):
-            gated(t)
-        scatter(pb[3], idx3, b3, 0, J)
-        scatter(pa[3], idx2, a3, 0, J)
+        pb.append(new_board("pb3", on="w2"))
 
         last = PACK - 1
-        rows_last = []
+        for t in range(last):
+            scatter(pb[t], idx3, b[t], 0, J)
+
+        def gate(t, cols, name):
+            g = tile([P, cols.stop - cols.start], F32, name)
+            nc.scalar.activation(out=g[:], in_=pb[t][:, cols], func=SIGMOID, bias=offset[:, t : t + 1], scale=slope[:, t : t + 1])
+            return g
+
+        gates = [gate(t, slice(0, C), "gate%d" % t) for t in range(last)]
+        pa.append(new_board("pa3", on="w1"))
+        scatter(pb[last], idx3, b[last], 0, J)
+        scatter(pa[last], idx2, a3, 0, J)
+
+        early_rows = tile([P, last, C], BF16, "early_rows")
+        for t in range(last):
+            nc.vector.tensor_tensor(out=early_rows[:, t, :], in0=pa[t][:], in1=gates[t][:], op=MULT)
+        chunks = [slice(i * CHUNK, (i + 1) * CHUNK) for i in range(CHUNKS)]
+        hid = [tile([P, CHUNK, PACK], BF16, "hid%d" % i) for i in range(CHUNKS)]
+        for i in range(CHUNKS):
+            nc.vector.tensor_copy(out=hid[i][:, :, 0:last], in_=early_rows[:, :, chunks[i]].rearrange("p t c -> p c t"))
+
+        last_rows = tile([P, C], BF16, "last_rows", on="early_rows")
 
         def last_row(i):
-            c0, c1 = CHUNKS[i]
-            g = tile([P, c1 - c0], F32, "gate_last%d" % i)
-            nc.scalar.activation(
-                out=g[:], in_=pb[last][:, c0:c1], func=SIGMOID, bias=offset[:, last : last + 1], scale=slope[:, last : last + 1]
-            )
-            row = tile([P, c1 - c0], BF16, "row%d" % i)
-            nc.vector.tensor_tensor(out=row[:], in0=pa[last][:, c0:c1], in1=g[:], op=MULT)
-            rows_last.append(row)
+            g = gate(last, chunks[i], "last_gate%d" % i)
+            nc.vector.tensor_tensor(out=last_rows[:, chunks[i]], in0=pa[last][:, chunks[i]], in1=g[:], op=MULT)
 
         def weave(i):
-            nc.vector.tensor_copy(out=hid[i][:, :, last], in_=rows_last[i][:])
+            nc.vector.tensor_copy(out=hid[i][:, :, last], in_=last_rows[:, chunks[i]])
+
+        out_rows = out.rearrange("(u p) c -> p u c", p=P)
 
         def finish(i):
-            c0, c1 = CHUNKS[i]
-            codes = tile([P, c1 - c0], U32, "codes%d" % i)
-            scales = tile([P, c1 - c0], U8, "scales%d" % i)
+            codes = tile([P, CHUNK], U32, "codes%d" % i)
+            scales = tile([P, CHUNK], U8, "scales%d" % i)
             nc.vector.quantize_mx(out=codes[:].bitcast(E4M3), scales=scales[:], in_=hid[i][:].rearrange("p c t -> p (c t)"))
-            for u in range(N // P):
-                rows = slice(u * P, (u + 1) * P)
-                acc = psum.tile([P, c1 - c0], F32, name="out_acc%d_%d" % (i, u), tag="acc")
-                nc.tensor.matmul_mx(
-                    out=acc[:], lhsT=wb[:, rows].bitcast(E5M2), lhsT_scale=wbs[:, rows], rhs=codes[:].bitcast(E4M3), rhs_scale=scales[:],
-                    start=True, stop=True,
-                )
-                result = tile([P, c1 - c0], F32, "result%d_%d" % (i, u))
-                if i == len(CHUNKS) - 1 and u == 0:
-                    nc.vector.tensor_copy(out=result[:], in_=acc[:])
-                else:
-                    nc.scalar.copy(out=result[:], in_=acc[:])
-                queue = nc.scalar if (i == len(CHUNKS) - 1 and u == 1) else nc.sync
-                queue.dma_start(out=out[rows, c0:c1], in_=result[:])
+            if i < CHUNKS - 1:
+                parts = (((0, 1), nc.scalar.copy, nc.sync),)
+            else:
+                parts = (((0,), nc.vector.tensor_copy, nc.sync), ((1,), nc.scalar.copy, nc.scalar))
+            for halves_of_n, engine_copy, queue in parts:
+                u0, count = halves_of_n[0], len(halves_of_n)
+                acc = psum.tile([P, count, CHUNK], F32, name="out_acc%d_%d" % (i, u0), tag="acc")
+                for u in halves_of_n:
+                    rows = slice(u * P, (u + 1) * P)
+                    nc.tensor.matmul_mx(
+                        out=acc[:, u - u0, :], lhsT=wb[:, rows].bitcast(E5M2), lhsT_scale=wbs[:, rows],
+                        rhs=codes[:].bitcast(E4M3), rhs_scale=scales[:], start=True, stop=True,
+                    )
+                result = tile([P, count, CHUNK], F32, "result%d_%d" % (i, u0))
+                engine_copy(out=result[:], in_=acc[:])
+                queue.dma_start(out=out_rows[:, u0 : u0 + count, chunks[i]], in_=result[:])
 
-        last_row(0)
-        last_row(1)
-        weave(0)
-        last_row(2)
-        weave(1)
-        finish(0)
-        weave(2)
-        finish(1)
-        finish(2)
+        for step in range(CHUNKS + 2):
+            if step < CHUNKS:
+                last_row(step)
+            if 1 <= step <= CHUNKS:
+                weave(step - 1)
+            if step >= 2:
+                finish(step - 2)

@@ -45,9 +45,9 @@ def tile_list_gatedboards_kernel(
             nc.vector.memset(plane[:].bitcast(I32), 0)
             return plane
 
-        def load_plane(queue, plane, dram):
+        def load_plane(queues, plane, dram):
             for q in range(QUADS):
-                queue.dma_start(out=plane[32 * q : 32 * q + 4, :].bitcast(I32), in_=dram[0, 4 * q : 4 * q + 4, :].bitcast(I32))
+                queues[q * len(queues) // QUADS].dma_start(out=plane[32 * q : 32 * q + 4, :].bitcast(I32), in_=dram[0, 4 * q : 4 * q + 4, :].bitcast(I32))
 
         def load_list(dram, name):
             offsets = tile([P, J // 16], U16, name)
@@ -60,11 +60,11 @@ def tile_list_gatedboards_kernel(
         idx = load_list(offs, "idx")
         ws_rows = tile([4, QUADS, R // 4], I32, "ws_rows")
         nc.scalar.dma_start(out=ws_rows[:], in_=w_scales[0].bitcast(I32).rearrange("(q r) c -> r q c", r=4))
-        xw = tile([P, T], I32, "xw")
-        nc.scalar.dma_start(out=xw[:], in_=words_of(xt_words))
-        load_plane(nc.sync, xs, xt_scales)
         w_raw = tile([P, R], U16, "w_raw")
-        nc.sync.dma_start(out=w_raw[:].bitcast(I32), in_=w_words[0].bitcast(I32))
+        nc.scalar.dma_start(out=w_raw[:].bitcast(I32), in_=w_words[0].bitcast(I32))
+        load_plane((nc.sync, nc.scalar), xs, xt_scales)
+        xw = tile([P, T], I32, "xw")
+        nc.sync.dma_start(out=xw[:], in_=words_of(xt_words))
         zero = tile([P, 1], F32, "zero")
         nc.gpsimd.memset(zero[:], 0.0)
         unused = tile([P, 1], F32, "unused")
@@ -73,7 +73,7 @@ def tile_list_gatedboards_kernel(
         w2_raw = tile([P, R], I32, "w2_raw")
         nc.sync.dma_start(out=w2_raw[:], in_=words_of(w2_words))
         w2s_plane = zeroed_plane(R, "w2s_plane")
-        load_plane(nc.sync, w2s_plane, w2_scales)
+        load_plane((nc.sync,), w2s_plane, w2_scales)
         idx3 = load_list(offs3, "idx3")
         slope = tile([P, PACK], F32, "slope")
         nc.sync.dma_start(out=slope[:], in_=sg.rearrange("(p t) o -> p (t o)", t=PACK))
@@ -82,7 +82,7 @@ def tile_list_gatedboards_kernel(
         wb = tile([P, N], I32, "wb")
         nc.sync.dma_start(out=wb[:], in_=words_of(wb_words))
         wbs = zeroed_plane(N, "wbs")
-        load_plane(nc.sync, wbs, wb_scales)
+        load_plane((nc.sync,), wbs, wb_scales)
 
         def new_board(name, on=None):
             board = tile([P, C], F32, name, on)
@@ -109,8 +109,8 @@ def tile_list_gatedboards_kernel(
 
         def gather(j0, j1):
             entries = idx[:, j0 // 16 : j1 // 16]
-            nc.vector.tensor_copy(out=xg[:, j0:j1], in_=xw[:].bitcast(U32).indirect(entries))
             nc.vector.tensor_copy(out=xgs[:, j0:j1], in_=xs[:].indirect(entries))
+            nc.vector.tensor_copy(out=xg[:, j0:j1], in_=xw[:].bitcast(U32).indirect(entries))
 
         def sums(operands, j0, j1, name):
             acc = psum.tile([P, len(operands), j1 - j0], F32, name="acc_" + name, tag="acc")
@@ -140,7 +140,7 @@ def tile_list_gatedboards_kernel(
                 (a,) = products([(w_lo[t][:, 0, :].bitcast(E2M1), ws_lo[:, t, :])], j0, j1, "a%d_%d" % (t, j0))
                 scatter(pa[t], idx2, a, j0, j1)
 
-        ws_hi = deal(nc.vector.tensor_copy, ws_plane, U8, "ws_hi", 2, 4, on="xs")
+        ws_hi = deal(nc.vector.tensor_copy, ws_plane, U8, "ws_hi", 2, 4, on="xw")
         pa.append(new_board("pa2", on="w0"))
         a2, a3 = products([(w_hi[:, u, :].bitcast(E2M1), ws_hi[:, u, :]) for u in range(2)], 0, J, "a23")
         scatter(pa[2], idx2, a2, 0, J)
@@ -150,7 +150,7 @@ def tile_list_gatedboards_kernel(
             out=w2[:].rearrange("p t (g i) -> p g t i", i=4), in_=w2_raw[:].rearrange("p (g i t) -> p g t i", i=4, t=PACK)
         )
         w2s = deal(nc.vector.tensor_copy, w2s_plane, U8, "w2s", 0, PACK)
-        pb = [new_board("pb%d" % t, on=on) for t, on in enumerate(("w1", "w_hi", "xs"))]
+        pb = [new_board("pb%d" % t, on=on) for t, on in enumerate(("w1", "w_hi", "xw"))]
         b = []
         for t in (0, 2):
             b.extend(products([(w2[:, t + u, :].bitcast(E5M2), w2s[:, t + u, :]) for u in range(2)], 0, J, "b%d" % t))
@@ -186,7 +186,8 @@ def tile_list_gatedboards_kernel(
             nc.vector.tensor_tensor(out=last_rows[:, chunks[i]], in0=pa[last][:, chunks[i]], in1=g[:], op=MULT)
 
         def weave(i):
-            nc.vector.tensor_copy(out=hid[i][:, :, last], in_=last_rows[:, chunks[i]])
+            engine_copy = nc.scalar.copy if 0 < i < CHUNKS - 1 else nc.vector.tensor_copy
+            engine_copy(out=hid[i][:, :, last], in_=last_rows[:, chunks[i]])
 
         out_rows = out.rearrange("(u p) c -> p u c", p=P)
 
@@ -194,7 +195,7 @@ def tile_list_gatedboards_kernel(
             codes = tile([P, CHUNK], U32, "codes%d" % i)
             scales = tile([P, CHUNK], U8, "scales%d" % i)
             nc.vector.quantize_mx(out=codes[:].bitcast(E4M3), scales=scales[:], in_=hid[i][:].rearrange("p c t -> p (c t)"))
-            if i < CHUNKS - 1:
+            if i != 2:
                 parts = (((0, 1), nc.scalar.copy, nc.sync),)
             else:
                 parts = (((0,), nc.vector.tensor_copy, nc.sync), ((1,), nc.scalar.copy, nc.scalar))
@@ -211,10 +212,9 @@ def tile_list_gatedboards_kernel(
                 engine_copy(out=result[:], in_=acc[:])
                 queue.dma_start(out=out_rows[:, u0 : u0 + count, chunks[i]], in_=result[:])
 
-        for step in range(CHUNKS + 2):
-            if step < CHUNKS:
-                last_row(step)
-            if 1 <= step <= CHUNKS:
-                weave(step - 1)
-            if step >= 2:
-                finish(step - 2)
+        for i in range(CHUNKS):
+            last_row(i)
+        for i in range(CHUNKS):
+            weave(i)
+        for i in (0, 1, 3, 2):
+            finish(i)

from contextlib import ExitStack

import concourse.mybir as mybir

K, T, J, R, C, N = 512, 1024, 256, 512, 512, 256
FLOPS = 2 * (2 * K * R * J + R * N * C)

F32 = mybir.dt.float32
BF16 = mybir.dt.bfloat16
I32 = mybir.dt.int32
U32 = mybir.dt.uint32
U16 = mybir.dt.uint16
U8 = mybir.dt.uint8
E4M3 = mybir.dt.float8_e4m3fn_x4
E5M2 = mybir.dt.float8_e5m2_x4
E2M1 = mybir.dt.float4_e2m1fn_x4
COPY = mybir.ActivationFunctionType.Copy
SIGMOID = mybir.ActivationFunctionType.Sigmoid
MULT = mybir.AluOpType.mult

P = 128
PACK = 4
QUADS = 4
HALF = J // 2
CHUNK = 128
CHUNKS = C // CHUNK


def tile_list_gatedboards_kernel(
    tc, xt_words, xt_scales, w_words, w_scales, w2_words, w2_scales, sg, bg, wb_words, wb_scales, offs, offs2, offs3, out
):
    nc = tc.nc
    with ExitStack() as ctx:
        keep = ctx.enter_context(tc.tile_pool(name="keep", bufs=1))
        psum = ctx.enter_context(tc.psum_pool(name="psum", bufs=8))

        def tile(shape, dtype, name, on=None):
            return keep.tile(shape, dtype, name=name, tag=on or name, align_bytes=64)

        def words_of(dram):
            return dram[0].rearrange("p c r -> p (c r)").bitcast(I32)

        def zeroed_plane(width, name):
            plane = tile([P, width], U8, name)
            nc.vector.memset(plane[:].bitcast(I32), 0)
            return plane

        def load_plane(queues, plane, dram):
            for q in range(QUADS):
                queues[q * len(queues) // QUADS].dma_start(out=plane[32 * q : 32 * q + 4, :].bitcast(I32), in_=dram[0, 4 * q : 4 * q + 4, :].bitcast(I32))

        def load_list(dram, name):
            offsets = tile([P, J // 16], U16, name)
            nc.sync.dma_start(out=offsets[:], in_=dram)
            return offsets

        xs = zeroed_plane(T, "xs")
        ws_two = zeroed_plane(2 * R, "ws_two")

        idx = load_list(offs, "idx")
        ws_rows = tile([4, QUADS, R // 4], I32, "ws_rows")
        nc.scalar.dma_start(out=ws_rows[:], in_=w_scales[0].bitcast(I32).rearrange("(q r) c -> r q c", r=4))
        w_raw = tile([P, R], U16, "w_raw")
        nc.scalar.dma_start(out=w_raw[:].bitcast(I32), in_=w_words[0].bitcast(I32))
        load_plane((nc.sync, nc.scalar), xs, xt_scales)
        xw = tile([P, T], I32, "xw")
        nc.sync.dma_start(out=xw[:], in_=words_of(xt_words))
        zero = tile([P, 1], F32, "zero")
        nc.gpsimd.memset(zero[:], 0.0)
        unused = tile([P, 1], F32, "unused")
        nc.scalar.activation(out=unused[:], in_=zero[:], func=SIGMOID)
        idx2 = load_list(offs2, "idx2")
        w2_raw = tile([P, R], I32, "w2_raw")
        nc.sync.dma_start(out=w2_raw[:], in_=words_of(w2_words))
        w2s_plane = zeroed_plane(R, "w2s_plane")
        load_plane((nc.sync,), w2s_plane, w2_scales)
        idx3 = load_list(offs3, "idx3")
        slope = tile([P, PACK], F32, "slope")
        nc.sync.dma_start(out=slope[:], in_=sg.rearrange("(p t) o -> p (t o)", t=PACK))
        offset = tile([P, PACK], F32, "offset")
        nc.sync.dma_start(out=offset[:], in_=bg.rearrange("(p t) o -> p (t o)", t=PACK))
        wb = tile([P, N], I32, "wb")
        nc.sync.dma_start(out=wb[:], in_=words_of(wb_words))
        wbs = zeroed_plane(N, "wbs")
        load_plane((nc.sync,), wbs, wb_scales)

        def new_board(name, on=None):
            board = tile([P, C], F32, name, on)
            nc.vector.memset(board[:], 0.0)
            return board


        def deal(engine_copy, raw, dtype, name, t0, t1, on=None):
            dealt = tile([P, t1 - t0, P], dtype, name, on)
            engine_copy(out=dealt[:], in_=raw[:].rearrange("p (m t) -> p t m", t=PACK)[:, t0:t1, :])
            return dealt

        ws_words = ws_two[:].bitcast(I32).rearrange("p (h c) -> p h c", h=2)
        for low in range(2):
            nc.vector.tensor_copy(out=ws_words[32 * low : 32 * low + 4, :, :], in_=ws_rows[:, low:QUADS:2, :])
        nc.vector.tensor_copy(out=ws_words[64:128, 0, :], in_=ws_words[0:64, 1, :])
        ws_plane = ws_two[:, 0:R]
        w_lo = [deal(nc.scalar.copy, w_raw, U16, "w%d" % t, t, t + 1) for t in range(2)]
        ws_lo = deal(nc.vector.tensor_copy, ws_plane, U8, "ws_lo", 0, 2)
        w_hi = deal(nc.scalar.copy, w_raw, U16, "w_hi", 2, 4)

        xg = tile([P, J], U32, "xg")
        xgs = tile([P, J], U8, "xgs")

        def gather(j0, j1):
            entries = idx[:, j0 // 16 : j1 // 16]
            nc.vector.tensor_copy(out=xgs[:, j0:j1], in_=xs[:].indirect(entries))
            nc.vector.tensor_copy(out=xg[:, j0:j1], in_=xw[:].bitcast(U32).indirect(entries))

        def sums(operands, j0, j1, name):
            acc = psum.tile([P, len(operands), j1 - j0], F32, name="acc_" + name, tag="acc")
            for u, (words, scales) in enumerate(operands):
                nc.tensor.matmul_mx(
                    out=acc[:, u, :], lhsT=words, lhsT_scale=scales, rhs=xg[:, j0:j1].bitcast(E4M3), rhs_scale=xgs[:, j0:j1],
                    start=True, stop=True,
                )
            return acc

        def leave_psum(acc, name):
            result = tile(list(acc.shape), F32, name)
            nc.vector.tensor_copy(out=result[:], in_=acc[:])
            return [result[:, u, :] for u in range(acc.shape[1])]

        def products(operands, j0, j1, name):
            return leave_psum(sums(operands, j0, j1, name), name)

        def scatter(board, offsets, values, j0, j1):
            nc.scalar.activation(out=board[:].indirect(offsets[:, j0 // 16 : j1 // 16]), in_=values, func=COPY)

        halves = ((0, HALF), (HALF, J))
        pa = [new_board("pa0"), new_board("pa1")]
        for j0, j1 in halves:
            gather(j0, j1)
            for t in range(2):
                (a,) = products([(w_lo[t][:, 0, :].bitcast(E2M1), ws_lo[:, t, :])], j0, j1, "a%d_%d" % (t, j0))
                scatter(pa[t], idx2, a, j0, j1)

        ws_hi = deal(nc.vector.tensor_copy, ws_plane, U8, "ws_hi", 2, 4, on="xw")
        pa.append(new_board("pa2", on="w0"))
        a2, a3 = products([(w_hi[:, u, :].bitcast(E2M1), ws_hi[:, u, :]) for u in range(2)], 0, J, "a23")
        scatter(pa[2], idx2, a2, 0, J)

        w2 = tile([P, PACK, P], I32, "w2")
        nc.vector.tensor_copy(
            out=w2[:].rearrange("p t (g i) -> p g t i", i=4), in_=w2_raw[:].rearrange("p (g i t) -> p g t i", i=4, t=PACK)
        )
        w2s = deal(nc.vector.tensor_copy, w2s_plane, U8, "w2s", 0, PACK)
        pb = [new_board("pb%d" % t, on=on) for t, on in enumerate(("w1", "w_hi", "xw"))]
        b = []
        for t in (0, 2):
            b.extend(products([(w2[:, t + u, :].bitcast(E5M2), w2s[:, t + u, :]) for u in range(2)], 0, J, "b%d" % t))

        pb.append(new_board("pb3", on="w2"))

        last = PACK - 1
        for t in range(last):
            scatter(pb[t], idx3, b[t], 0, J)

        def gate(t, cols, name):
            g = tile([P, cols.stop - cols.start], F32, name)
            nc.scalar.activation(out=g[:], in_=pb[t][:, cols], func=SIGMOID, bias=offset[:, t : t + 1], scale=slope[:, t : t + 1])
            return g

        gates = [gate(t, slice(0, C), "gate%d" % t) for t in range(last)]
        pa.append(new_board("pa3", on="w1"))
        scatter(pb[last], idx3, b[last], 0, J)
        scatter(pa[last], idx2, a3, 0, J)

        early_rows = tile([P, last, C], BF16, "early_rows")
        for t in range(last):
            nc.vector.tensor_tensor(out=early_rows[:, t, :], in0=pa[t][:], in1=gates[t][:], op=MULT)
        chunks = [slice(i * CHUNK, (i + 1) * CHUNK) for i in range(CHUNKS)]
        hid = [tile([P, CHUNK, PACK], BF16, "hid%d" % i) for i in range(CHUNKS)]
        for i in range(CHUNKS):
            nc.vector.tensor_copy(out=hid[i][:, :, 0:last], in_=early_rows[:, :, chunks[i]].rearrange("p t c -> p c t"))

        last_rows = tile([P, C], BF16, "last_rows", on="early_rows")

        def last_row(i):
            g = gate(last, chunks[i], "last_gate%d" % i)
            nc.vector.tensor_tensor(out=last_rows[:, chunks[i]], in0=pa[last][:, chunks[i]], in1=g[:], op=MULT)

        def weave(i):
            engine_copy = nc.scalar.copy if 0 < i < CHUNKS - 1 else nc.vector.tensor_copy
            engine_copy(out=hid[i][:, :, last], in_=last_rows[:, chunks[i]])

        out_rows = out.rearrange("(u p) c -> p u c", p=P)

        def finish(i):
            codes = tile([P, CHUNK], U32, "codes%d" % i)
            scales = tile([P, CHUNK], U8, "scales%d" % i)
            nc.vector.quantize_mx(out=codes[:].bitcast(E4M3), scales=scales[:], in_=hid[i][:].rearrange("p c t -> p (c t)"))
            if i != 2:
                parts = (((0, 1), nc.scalar.copy, nc.sync),)
            else:
                parts = (((0,), nc.vector.tensor_copy, nc.sync), ((1,), nc.scalar.copy, nc.scalar))
            for halves_of_n, engine_copy, queue in parts:
                u0, count = halves_of_n[0], len(halves_of_n)
                acc = psum.tile([P, count, CHUNK], F32, name="out_acc%d_%d" % (i, u0), tag="acc")
                for u in halves_of_n:
                    rows = slice(u * P, (u + 1) * P)
                    nc.tensor.matmul_mx(
                        out=acc[:, u - u0, :], lhsT=wb[:, rows].bitcast(E5M2), lhsT_scale=wbs[:, rows],
                        rhs=codes[:].bitcast(E4M3), rhs_scale=scales[:], start=True, stop=True,
                    )
                result = tile([P, count, CHUNK], F32, "result%d_%d" % (i, u0))
                engine_copy(out=result[:], in_=acc[:])
                queue.dma_start(out=out_rows[:, u0 : u0 + count, chunks[i]], in_=result[:])

        for i in range(CHUNKS):
            last_row(i)
        for i in range(CHUNKS):
            weave(i)
        for i in (0, 1, 3, 2):
            finish(i)
